import numpy as np
CORES = [1,129,9,137,17,145,25,153,33,161,41,169,49,177,57,185,65,193,73,201,81,209,89,217,97,225,105,233,113,241,121,249]
N = 32
COUNTS = [[0,0,8,0,0,8,8,64,0,8,16,8,0,0,0,16,8,8,0,16,0,8,16,16,16,16,8,8,8,16,8,8],[0,0,0,16,8,0,0,64,16,0,0,8,16,8,0,0,0,8,8,8,16,16,8,0,16,8,16,0,16,0,8,8],[16,8,0,8,0,0,0,64,8,0,0,16,8,16,8,8,16,8,16,0,8,0,0,0,8,16,8,8,0,16,16,16],[0,8,0,0,16,0,8,64,8,16,8,16,0,8,8,0,0,0,8,8,8,8,16,8,8,16,8,16,16,0,16,0],[16,8,16,0,0,8,8,64,16,8,0,8,8,8,16,8,0,16,0,0,0,0,0,0,0,16,8,16,0,16,16,16],[16,8,0,8,0,0,8,64,0,16,16,16,8,0,8,16,16,8,0,0,0,8,16,8,16,16,0,8,0,16,8,16],[8,8,8,0,8,0,0,64,8,8,8,8,0,16,0,0,8,8,0,16,0,0,0,8,16,16,16,16,8,8,8,8],[0,0,16,0,8,8,0,0,0,16,8,8,8,8,8,8,0,8,0,16,0,16,0,16,0,16,8,16,8,16,8,16],[8,0,16,8,16,16,0,64,0,0,8,0,16,16,0,0,16,16,8,8,8,8,8,0,16,0,8,8,16,16,16,8],[0,0,16,0,0,8,0,64,16,0,8,0,16,8,0,16,8,8,0,8,16,0,8,0,0,8,16,8,16,8,16,16],[0,8,8,0,0,8,8,64,8,16,0,0,16,16,0,8,8,8,8,8,8,8,16,16,16,0,8,8,0,8,8,8],[16,16,0,8,0,0,16,64,16,0,0,0,8,16,8,8,16,8,16,16,0,0,8,8,16,0,16,8,0,16,8,8],[8,16,0,16,16,16,0,64,8,16,8,16,0,0,8,0,8,8,0,8,16,16,0,8,8,0,0,8,8,8,16,0],[0,0,16,16,8,8,16,64,16,16,0,8,0,0,16,8,16,8,8,16,0,8,16,0,8,16,0,16,8,0,16,16],[8,16,8,16,0,8,0,64,0,0,16,8,8,0,0,0,0,0,16,8,8,0,8,0,0,16,8,0,16,0,0,16],[8,16,0,8,8,0,16,64,0,8,0,0,8,8,0,0,16,16,8,16,0,16,0,0,0,16,16,0,8,0,0,16],[0,8,8,8,8,8,8,64,16,0,16,8,0,16,0,16,0,0,16,0,0,16,8,16,16,8,16,8,16,0,8,8],[8,16,8,8,0,0,8,64,0,0,8,8,0,0,0,0,0,0,0,8,0,0,16,0,8,8,0,0,0,16,16,16],[16,16,8,0,0,16,8,64,8,16,0,0,8,8,0,8,8,8,0,16,16,0,0,8,0,16,16,0,8,16,16,0],[0,0,0,0,0,16,0,64,8,0,16,0,16,8,8,8,16,16,8,0,16,0,0,8,8,0,16,8,0,16,8,16],[8,8,0,8,0,0,0,64,0,8,8,0,0,16,16,0,8,0,8,0,0,0,0,16,16,8,8,8,16,16,16,8],[0,16,0,16,8,8,16,64,8,8,0,16,0,8,0,8,8,8,8,0,0,0,16,8,16,16,8,0,8,16,8,0],[16,8,0,8,16,8,0,64,8,8,0,8,8,8,16,0,8,16,0,8,8,0,0,8,8,16,8,16,16,16,8,0],[16,8,16,0,16,8,8,64,8,0,16,8,16,8,0,16,0,16,0,8,0,8,8,0,8,0,0,16,8,0,8,0],[0,8,0,8,0,0,16,64,8,16,0,16,0,16,16,16,8,0,8,16,8,16,16,8,0,8,16,8,0,8,0,16],[0,0,0,0,16,16,16,64,0,8,16,8,16,8,8,8,16,16,0,8,16,8,16,0,0,0,8,8,8,16,0,8],[0,8,8,8,0,16,0,64,8,16,16,0,16,0,8,8,8,8,0,0,16,16,16,0,16,16,0,16,16,8,0,16],[0,16,0,16,8,16,8,64,8,0,16,0,0,16,16,16,0,16,16,16,16,0,8,8,0,8,16,0,16,16,8,8],[0,0,0,16,0,16,16,64,0,0,16,16,8,8,0,8,0,0,16,8,0,0,0,8,8,8,0,8,0,16,0,16],[16,0,16,0,16,16,16,64,0,8,0,8,16,0,16,8,16,16,0,16,16,8,16,0,0,16,8,8,0,0,16,16],[0,16,8,16,0,8,16,64,8,8,16,16,16,8,8,0,16,8,8,0,16,16,16,16,0,16,0,0,0,16,0,8],[8,16,0,16,16,8,8,64,8,8,8,16,8,8,0,8,0,0,16,0,16,0,8,16,8,0,8,16,0,0,8,0]]
XW, YW = 352, 1984
def setup_inputs(rng):
    return {"x": rng.standard_normal((N, 128, XW), dtype=np.float32)}
def reference(x):
    y = np.full((N, 128, YW), np.nan, x.dtype)
    fill = [0] * N
    for s in range(N):
        o = 0
        for d in range(N):
            c = COUNTS[s][d]
            y[d][:, fill[d]:fill[d] + c] = x[s][:, o:o + c]
            o += c; fill[d] += c
    return {"y": y}

@@ -1,0 +1,44 @@
+SCRATCH = {
+    "xs": ("sbuf", [128, 352], "float32"),
+    "land": ("sbuf", [128, 1984], "float32"),
+}
+SEMAPHORES = ["loaded", "handed", "sent", "arrived", "stored"]
+
+
+def rank_program(g, core, T, topo):
+    counts = T.tables["COUNTS"]
+    n = len(counts)
+    cores = T.cores
+    rank = T.rank_of(core)
+    owner = T.rank_of(core - 1) if core % 8 == 2 else None
+    if rank is None and owner is None:
+        return
+    s = rank if rank is not None else owner
+    tot = sum(counts[s])
+    sent = 0
+    if rank is not None:
+        g.dma_start(T.xs[:, 0:tot], T.x[:, 0:tot]).then_inc(T.sem.loaded, 16)
+        g.wait_ge(T.sem.loaded, 16)
+        rid, pid = topo.addr(core + 1, core)
+        g.remote_dma(T.xs[:, 0:tot], T.xs[:, 0:tot], T.sem.handed, T.sem.sent, pid, rid, 0xFFFF)
+        sent += 16
+    else:
+        g.wait_ge(T.sem.handed, 16)
+    o = 0
+    for d in range(n):
+        c = counts[s][d]
+        if c and d != s:
+            same = topo.chip(cores[d]) % 2 == topo.chip(core) % 2
+            if same == (rank is not None):
+                off = sum(counts[q][d] for q in range(s))
+                rid, pid = topo.addr(cores[d], core)
+                g.remote_dma(T.land[:, off:off + c], T.xs[:, o:o + c], T.sem.arrived, T.sem.sent, pid, rid, 0xFF)
+                sent += 8
+        o += c
+    g.wait_ge(T.sem.sent, sent)
+    if rank is not None:
+        inc = 8 * sum(1 for q in range(n) if q != s and counts[q][s])
+        g.wait_ge(T.sem.arrived, inc)
+        w = sum(counts[q][s] for q in range(n))
+        g.dma_start(T.y[:, 0:w], T.land[:, 0:w]).then_inc(T.sem.stored, 16)
+        g.wait_ge(T.sem.stored, 16)

@@ -2,43 +2,136 @@ SCRATCH = {
     "xs": ("sbuf", [128, 352], "float32"),
     "land": ("sbuf", [128, 1984], "float32"),
 }
-SEMAPHORES = ["loaded", "handed", "sent", "arrived", "stored"]
+SEMAPHORES = ["loaded", "handed", "sent", "arr0", "arr1", "arr2", "arr3", "rel0", "rel1", "stored_a", "stored_b"]
+
+PIECES = 4
+DIE1, DIE0 = (2, 3), (6, 7)
+
+
+def chunks(items, k):
+    out, at = [], 0
+    for i in range(k):
+        size = (len(items) - at + (k - i - 1)) // (k - i)
+        out.append(items[at:at + size])
+        at += size
+    return out
+
+
+def make_plan(counts, cores, topo):
+    n = len(counts)
+    xo = [[sum(counts[s][:d]) for d in range(n)] for s in range(n)]
+    yo = [[sum(counts[q][d] for q in range(s)) for d in range(n)] for s in range(n)]
+    par = [topo.chip(c) % 2 for c in cores]
+    hot = max(range(n), key=lambda d: sum(counts[s][d] for s in range(n)))
+    mrank = [r for r in range(n) if topo.mates(cores[r], cores[hot])][0]
+    mbase = cores[mrank] - cores[mrank] % 8
+
+    same = [s for s in range(n) if s != hot and counts[s][hot] and par[s] == par[hot]]
+    other = [s for s in range(n) if s != mrank and counts[s][hot] and par[s] != par[hot]]
+    third = (len(same) + len(other)) // 3
+    runs = []
+    for s in other:
+        if 2 * len(runs) + 2 <= third and s + 1 in other and not (runs and runs[-1][1] == s):
+            runs.append((s, s + 1))
+    via_m = [s for r in runs for s in r]
+    straight = [s for s in other if s not in via_m]
+    busy = [r for r in same if any(topo.mates(cores[r], cores[q]) for q in straight)]
+    need0 = max(0, (len(same) + len(straight)) // 2 - len(straight))
+    same0 = [s for s in same if s not in busy][:need0]
+    own = via_m + [s for s in same if s not in same0]
+    relay_cores = [DIE1[0], DIE0[0], DIE1[1], DIE0[1]]
+    relay = {}
+    for i, r in enumerate(runs):
+        for s in r:
+            relay[s] = (mbase + relay_cores[i % 4], "rel%d" % (i // 4))
+
+    def arr(s, d):
+        return "arr%d" % (s * PIECES // n) if d == hot else "arr0"
+
+    writes = {}
+    for s in range(n):
+        c = cores[s]
+        base = c - c % 8
+        mine = writes.setdefault(c, [])
+        if s in own:
+            w = counts[s][hot]
+            if s in relay:
+                mine.append(("loaded", relay[s][0], "land", yo[s][hot], "xs", xo[s][hot], w, relay[s][1], 8))
+            else:
+                mine.append(("loaded", cores[hot], "land", yo[s][hot], "xs", xo[s][hot], w, arr(s, hot), 8))
+        todo = [d for d in range(n) if d != s and counts[s][d] and not (d == hot and s in own)]
+        parts = chunks(todo, 4)
+        die0 = [i for i in range(4) if mrank in parts[i] or hot in parts[i]]
+        free = [i for i in range(4) if i not in die0]
+        while len(die0) < 2:
+            die0.append(free.pop(s // 2 % len(free)))
+        die0.sort()
+        helper = {}
+        for k, i in enumerate(die0):
+            helper[i] = base + DIE0[k]
+        for k, i in enumerate(free):
+            helper[i] = base + DIE1[k]
+        order = sorted(range(4), key=lambda i: 0 if hot in parts[i] else 1)
+        for i in order:
+            if not parts[i]:
+                continue
+            lo, hi = xo[s][parts[i][0]], xo[s][parts[i][-1]] + counts[s][parts[i][-1]]
+            mine.append(("loaded", helper[i], "xs", lo, "xs", lo, hi - lo, "handed", 16))
+            hw = writes.setdefault(helper[i], [])
+            for d in sorted(parts[i], key=lambda d: -counts[s][d]):
+                hw.append(("handed", cores[d], "land", yo[s][d], "xs", xo[s][d], counts[s][d], arr(s, d), 8))
+    for r in runs:
+        rc, sem = relay[r[0]]
+        lo = yo[r[0]][hot]
+        w = counts[r[0]][hot] + counts[r[1]][hot]
+        writes.setdefault(rc, []).append((sem, cores[hot], "land", lo, "land", lo, w, arr(r[0], hot), 8))
+
+    reach = {}
+    for c in writes:
+        for (after, dst, db, dc, sb, sc, w, sem, eng) in writes[c]:
+            reach[(dst, sem)] = reach.get((dst, sem), 0) + eng
+    return writes, reach, hot
+
+
+CACHE = {}
 
 
 def rank_program(g, core, T, topo):
+    if "plan" not in CACHE:
+        CACHE["plan"] = make_plan(T.tables["COUNTS"], T.cores, topo)
+    writes, reach, hot = CACHE["plan"]
     counts = T.tables["COUNTS"]
     n = len(counts)
-    cores = T.cores
     rank = T.rank_of(core)
-    owner = T.rank_of(core - 1) if core % 8 == 2 else None
-    if rank is None and owner is None:
+    if rank is None and core not in writes:
         return
-    s = rank if rank is not None else owner
-    tot = sum(counts[s])
+
+    if rank is not None:
+        tot = sum(counts[rank])
+        g.sync.dma_start(T.xs[:, 0:tot], T.x[:, 0:tot]).then_inc(T.sem.loaded, 16)
+
+    waited = []
     sent = 0
+    for (after, dst, db, dc, sb, sc, w, sem, eng) in writes.get(core, []):
+        if after not in waited:
+            g.wait_ge(T.sem[after], 16 if after == "loaded" else reach[(core, after)])
+            waited.append(after)
+        rid, pid = topo.addr(dst, core)
+        g.remote_dma(T[db][:, dc:dc + w], T[sb][:, sc:sc + w], T.sem[sem], T.sem.sent, pid, rid, (1 << eng) - 1)
+        sent += eng
+    if sent:
+        g.wait_ge(T.sem.sent, sent)
+
     if rank is not None:
-        g.dma_start(T.xs[:, 0:tot], T.x[:, 0:tot]).then_inc(T.sem.loaded, 16)
-        g.wait_ge(T.sem.loaded, 16)
-        rid, pid = topo.addr(core + 1, core)
-        g.remote_dma(T.xs[:, 0:tot], T.xs[:, 0:tot], T.sem.handed, T.sem.sent, pid, rid, 0xFFFF)
-        sent += 16
-    else:
-        g.wait_ge(T.sem.handed, 16)
-    o = 0
-    for d in range(n):
-        c = counts[s][d]
-        if c and d != s:
-            same = topo.chip(cores[d]) % 2 == topo.chip(core) % 2
-            if same == (rank is not None):
-                off = sum(counts[q][d] for q in range(s))
-                rid, pid = topo.addr(cores[d], core)
-                g.remote_dma(T.land[:, off:off + c], T.xs[:, o:o + c], T.sem.arrived, T.sem.sent, pid, rid, 0xFF)
-                sent += 8
-        o += c
-    g.wait_ge(T.sem.sent, sent)
-    if rank is not None:
-        inc = 8 * sum(1 for q in range(n) if q != s and counts[q][s])
-        g.wait_ge(T.sem.arrived, inc)
-        w = sum(counts[q][s] for q in range(n))
-        g.dma_start(T.y[:, 0:w], T.land[:, 0:w]).then_inc(T.sem.stored, 16)
-        g.wait_ge(T.sem.stored, 16)
+        k = PIECES if rank == hot else 1
+        issued = [0, 0]
+        for p in range(k):
+            lo = sum(counts[q][rank] for q in range(p * n // k))
+            hi = sum(counts[q][rank] for q in range((p + 1) * n // k))
+            q = (g.sync, g.scalar)[p % 2]
+            q.wait_ge(T.sem["arr%d" % p], reach[(core, "arr%d" % p)])
+            q.dma_start(T.y[:, lo:hi], T.land[:, lo:hi]).then_inc((T.sem.stored_a, T.sem.stored_b)[p % 2], 16)
+            issued[p % 2] += 16
+        g.sync.wait_ge(T.sem.stored_a, issued[0])
+        if issued[1]:
+            g.scalar.wait_ge(T.sem.stored_b, issued[1])

@@ -2,18 +2,34 @@ SCRATCH = {
     "xs": ("sbuf", [128, 352], "float32"),
     "land": ("sbuf", [128, 1984], "float32"),
 }
-SEMAPHORES = ["loaded", "handed", "sent", "arr0", "arr1", "arr2", "arr3", "rel0", "rel1", "stored_a", "stored_b"]
+SEMAPHORES = ["loaded", "handed", "sent", "arr0", "arr1", "rel0", "rel1", "stored_a", "stored_b"]
 
-PIECES = 4
-DIE1, DIE0 = (2, 3), (6, 7)
+PIECES = 2
+HELPERS = (2, 3, 6, 7)
+ORDERS = [(a, b, c, d) for a in HELPERS for b in HELPERS for c in HELPERS for d in HELPERS
+          if len({a, b, c, d}) == 4]
 
 
-def chunks(items, k):
+def cut(items, busy):
+    load = list(busy)
+    for _ in items:
+        load[load.index(min(load))] += 1
     out, at = [], 0
-    for i in range(k):
-        size = (len(items) - at + (k - i - 1)) // (k - i)
-        out.append(items[at:at + size])
-        at += size
+    for i in range(len(busy)):
+        out.append(items[at:at + load[i] - busy[i]])
+        at += load[i] - busy[i]
+    return out
+
+
+def links(topo, src, dst):
+    at, to, die = (topo.host(src), topo.chip(src)), (topo.host(dst), topo.chip(dst)), topo.die(src)
+    out = []
+    if at[1] % 2 != to[1] % 2:
+        out.append(("mate", at, die))
+        at = (at[0], at[1] ^ 1)
+    if at != to:
+        out.append(("out", at, die))
+        out.append(("in", to, die))
     return out
 
 
@@ -39,47 +55,61 @@ def make_plan(counts, cores, topo):
     need0 = max(0, (len(same) + len(straight)) // 2 - len(straight))
     same0 = [s for s in same if s not in busy][:need0]
     own = via_m + [s for s in same if s not in same0]
-    relay_cores = [DIE1[0], DIE0[0], DIE1[1], DIE0[1]]
     relay = {}
+    passes = {}
     for i, r in enumerate(runs):
+        rc = mbase + (2, 6, 3, 7)[i % 4]
+        passes[rc] = passes.get(rc, 0) + 1
         for s in r:
-            relay[s] = (mbase + relay_cores[i % 4], "rel%d" % (i // 4))
+            relay[s] = (rc, "rel%d" % (i // 4))
 
     def arr(s, d):
         return "arr%d" % (s * PIECES // n) if d == hot else "arr0"
 
+    load = {}
+
+    def charge(src, dst, w):
+        for k in links(topo, src, dst):
+            load[k] = load.get(k, 0) + w
+
     writes = {}
-    for s in range(n):
+    for s in own:
+        dst, sem = relay[s] if s in relay else (cores[hot], arr(s, hot))
+        writes[cores[s]] = [("loaded", dst, "land", yo[s][hot], "xs", xo[s][hot], counts[s][hot], sem, 8)]
+        charge(cores[s], dst, counts[s][hot])
+    for r in runs:
+        charge(relay[r[0]][0], cores[hot], counts[r[0]][hot] + counts[r[1]][hot])
+
+    for s in sorted(range(n), key=lambda r: r != mrank):
         c = cores[s]
         base = c - c % 8
-        mine = writes.setdefault(c, [])
-        if s in own:
-            w = counts[s][hot]
-            if s in relay:
-                mine.append(("loaded", relay[s][0], "land", yo[s][hot], "xs", xo[s][hot], w, relay[s][1], 8))
-            else:
-                mine.append(("loaded", cores[hot], "land", yo[s][hot], "xs", xo[s][hot], w, arr(s, hot), 8))
         todo = [d for d in range(n) if d != s and counts[s][d] and not (d == hot and s in own)]
-        parts = chunks(todo, 4)
-        die0 = [i for i in range(4) if mrank in parts[i] or hot in parts[i]]
-        free = [i for i in range(4) if i not in die0]
-        while len(die0) < 2:
-            die0.append(free.pop(s // 2 % len(free)))
-        die0.sort()
-        helper = {}
-        for k, i in enumerate(die0):
-            helper[i] = base + DIE0[k]
-        for k, i in enumerate(free):
-            helper[i] = base + DIE1[k]
-        order = sorted(range(4), key=lambda i: 0 if hot in parts[i] else 1)
-        for i in order:
-            if not parts[i]:
+        best = None
+        for order in ORDERS:
+            if s in own:
+                parts = [[d for d in todo if d < hot]] + cut([d for d in todo if d > hot], [0, 0, 0])
+            else:
+                parts = cut(todo, [passes.get(base + h, 0) for h in order])
+            if s != mrank and any(h < 4 and (mrank in p or hot in p) for h, p in zip(order, parts)):
                 continue
-            lo, hi = xo[s][parts[i][0]], xo[s][parts[i][-1]] + counts[s][parts[i][-1]]
-            mine.append(("loaded", helper[i], "xs", lo, "xs", lo, hi - lo, "handed", 16))
-            hw = writes.setdefault(helper[i], [])
-            for d in sorted(parts[i], key=lambda d: -counts[s][d]):
+            add = {}
+            for h, p in zip(order, parts):
+                for d in p:
+                    for k in links(topo, base + h, cores[d]):
+                        add[k] = add.get(k, 0) + counts[s][d]
+            cost = sum((load.get(k, 0) + add[k]) ** 2 - load.get(k, 0) ** 2 for k in add)
+            if best is None or cost < best[0]:
+                best = (cost, order, parts)
+        mine = writes.setdefault(c, [])
+        for h, p in sorted(zip(best[1], best[2]), key=lambda hp: hot not in hp[1]):
+            if not p:
+                continue
+            lo, hi = xo[s][p[0]], xo[s][p[-1]] + counts[s][p[-1]]
+            mine.append(("loaded", base + h, "xs", lo, "xs", lo, hi - lo, "handed", 16))
+            hw = writes.setdefault(base + h, [])
+            for d in sorted(p, key=lambda d: -counts[s][d]):
                 hw.append(("handed", cores[d], "land", yo[s][d], "xs", xo[s][d], counts[s][d], arr(s, d), 8))
+                charge(base + h, cores[d], counts[s][d])
     for r in runs:
         rc, sem = relay[r[0]]
         lo = yo[r[0]][hot]
@@ -124,14 +154,10 @@ def rank_program(g, core, T, topo):
 
     if rank is not None:
         k = PIECES if rank == hot else 1
-        issued = [0, 0]
         for p in range(k):
             lo = sum(counts[q][rank] for q in range(p * n // k))
             hi = sum(counts[q][rank] for q in range((p + 1) * n // k))
-            q = (g.sync, g.scalar)[p % 2]
+            q, done = ((g.sync, T.sem.stored_a), (g.scalar, T.sem.stored_b))[p]
             q.wait_ge(T.sem["arr%d" % p], reach[(core, "arr%d" % p)])
-            q.dma_start(T.y[:, lo:hi], T.land[:, lo:hi]).then_inc((T.sem.stored_a, T.sem.stored_b)[p % 2], 16)
-            issued[p % 2] += 16
-        g.sync.wait_ge(T.sem.stored_a, issued[0])
-        if issued[1]:
-            g.scalar.wait_ge(T.sem.stored_b, issued[1])
+            q.dma_start(T.y[:, lo:hi], T.land[:, lo:hi]).then_inc(done, 16)
+            q.wait_ge(done, 16)

SCRATCH = {
    "xs": ("sbuf", [128, 352], "float32"),
    "land": ("sbuf", [128, 1984], "float32"),
}
SEMAPHORES = ["loaded", "handed", "sent", "arr0", "arr1", "rel0", "rel1", "stored_a", "stored_b"]

PIECES = 2
HELPERS = (2, 3, 6, 7)
ORDERS = [(a, b, c, d) for a in HELPERS for b in HELPERS for c in HELPERS for d in HELPERS
          if len({a, b, c, d}) == 4]


def cut(items, busy):
    load = list(busy)
    for _ in items:
        load[load.index(min(load))] += 1
    out, at = [], 0
    for i in range(len(busy)):
        out.append(items[at:at + load[i] - busy[i]])
        at += load[i] - busy[i]
    return out


def links(topo, src, dst):
    at, to, die = (topo.host(src), topo.chip(src)), (topo.host(dst), topo.chip(dst)), topo.die(src)
    out = []
    if at[1] % 2 != to[1] % 2:
        out.append(("mate", at, die))
        at = (at[0], at[1] ^ 1)
    if at != to:
        out.append(("out", at, die))
        out.append(("in", to, die))
    return out


def make_plan(counts, cores, topo):
    n = len(counts)
    xo = [[sum(counts[s][:d]) for d in range(n)] for s in range(n)]
    yo = [[sum(counts[q][d] for q in range(s)) for d in range(n)] for s in range(n)]
    par = [topo.chip(c) % 2 for c in cores]
    hot = max(range(n), key=lambda d: sum(counts[s][d] for s in range(n)))
    mrank = [r for r in range(n) if topo.mates(cores[r], cores[hot])][0]
    mbase = cores[mrank] - cores[mrank] % 8

    same = [s for s in range(n) if s != hot and counts[s][hot] and par[s] == par[hot]]
    other = [s for s in range(n) if s != mrank and counts[s][hot] and par[s] != par[hot]]
    third = (len(same) + len(other)) // 3
    runs = []
    for s in other:
        if 2 * len(runs) + 2 <= third and s + 1 in other and not (runs and runs[-1][1] == s):
            runs.append((s, s + 1))
    via_m = [s for r in runs for s in r]
    straight = [s for s in other if s not in via_m]
    busy = [r for r in same if any(topo.mates(cores[r], cores[q]) for q in straight)]
    need0 = max(0, (len(same) + len(straight)) // 2 - len(straight))
    same0 = [s for s in same if s not in busy][:need0]
    own = via_m + [s for s in same if s not in same0]
    relay = {}
    passes = {}
    for i, r in enumerate(runs):
        rc = mbase + (2, 6, 3, 7)[i % 4]
        passes[rc] = passes.get(rc, 0) + 1
        for s in r:
            relay[s] = (rc, "rel%d" % (i // 4))

    def arr(s, d):
        return "arr%d" % (s * PIECES // n) if d == hot else "arr0"

    load = {}

    def charge(src, dst, w):
        for k in links(topo, src, dst):
            load[k] = load.get(k, 0) + w

    writes = {}
    for s in own:
        dst, sem = relay[s] if s in relay else (cores[hot], arr(s, hot))
        writes[cores[s]] = [("loaded", dst, "land", yo[s][hot], "xs", xo[s][hot], counts[s][hot], sem, 8)]
        charge(cores[s], dst, counts[s][hot])
    for r in runs:
        charge(relay[r[0]][0], cores[hot], counts[r[0]][hot] + counts[r[1]][hot])

    for s in sorted(range(n), key=lambda r: r != mrank):
        c = cores[s]
        base = c - c % 8
        todo = [d for d in range(n) if d != s and counts[s][d] and not (d == hot and s in own)]
        best = None
        for order in ORDERS:
            if s in own:
                parts = [[d for d in todo if d < hot]] + cut([d for d in todo if d > hot], [0, 0, 0])
            else:
                parts = cut(todo, [passes.get(base + h, 0) for h in order])
            if s != mrank and any(h < 4 and (mrank in p or hot in p) for h, p in zip(order, parts)):
                continue
            add = {}
            for h, p in zip(order, parts):
                for d in p:
                    for k in links(topo, base + h, cores[d]):
                        add[k] = add.get(k, 0) + counts[s][d]
            cost = sum((load.get(k, 0) + add[k]) ** 2 - load.get(k, 0) ** 2 for k in add)
            if best is None or cost < best[0]:
                best = (cost, order, parts)
        mine = writes.setdefault(c, [])
        for h, p in sorted(zip(best[1], best[2]), key=lambda hp: hot not in hp[1]):
            if not p:
                continue
            lo, hi = xo[s][p[0]], xo[s][p[-1]] + counts[s][p[-1]]
            mine.append(("loaded", base + h, "xs", lo, "xs", lo, hi - lo, "handed", 16))
            hw = writes.setdefault(base + h, [])
            for d in sorted(p, key=lambda d: -counts[s][d]):
                hw.append(("handed", cores[d], "land", yo[s][d], "xs", xo[s][d], counts[s][d], arr(s, d), 8))
                charge(base + h, cores[d], counts[s][d])
    for r in runs:
        rc, sem = relay[r[0]]
        lo = yo[r[0]][hot]
        w = counts[r[0]][hot] + counts[r[1]][hot]
        writes.setdefault(rc, []).append((sem, cores[hot], "land", lo, "land", lo, w, arr(r[0], hot), 8))

    reach = {}
    for c in writes:
        for (after, dst, db, dc, sb, sc, w, sem, eng) in writes[c]:
            reach[(dst, sem)] = reach.get((dst, sem), 0) + eng
    return writes, reach, hot


CACHE = {}


def rank_program(g, core, T, topo):
    if "plan" not in CACHE:
        CACHE["plan"] = make_plan(T.tables["COUNTS"], T.cores, topo)
    writes, reach, hot = CACHE["plan"]
    counts = T.tables["COUNTS"]
    n = len(counts)
    rank = T.rank_of(core)
    if rank is None and core not in writes:
        return

    if rank is not None:
        tot = sum(counts[rank])
        g.sync.dma_start(T.xs[:, 0:tot], T.x[:, 0:tot]).then_inc(T.sem.loaded, 16)

    waited = []
    sent = 0
    for (after, dst, db, dc, sb, sc, w, sem, eng) in writes.get(core, []):
        if after not in waited:
            g.wait_ge(T.sem[after], 16 if after == "loaded" else reach[(core, after)])
            waited.append(after)
        rid, pid = topo.addr(dst, core)
        g.remote_dma(T[db][:, dc:dc + w], T[sb][:, sc:sc + w], T.sem[sem], T.sem.sent, pid, rid, (1 << eng) - 1)
        sent += eng
    if sent:
        g.wait_ge(T.sem.sent, sent)

    if rank is not None:
        k = PIECES if rank == hot else 1
        for p in range(k):
            lo = sum(counts[q][rank] for q in range(p * n // k))
            hi = sum(counts[q][rank] for q in range((p + 1) * n // k))
            q, done = ((g.sync, T.sem.stored_a), (g.scalar, T.sem.stored_b))[p]
            q.wait_ge(T.sem["arr%d" % p], reach[(core, "arr%d" % p)])
            q.dma_start(T.y[:, lo:hi], T.land[:, lo:hi]).then_inc(done, 16)
            q.wait_ge(done, 16)
